import numpy as np
import ml_dtypes


def mxq(x, axis, fmt="e4m3"):
    dtype, down = {"e4m3": (ml_dtypes.float8_e4m3fn, 7), "e5m2": (ml_dtypes.float8_e5m2, 14)}[fmt]
    v = np.moveaxis(np.asarray(x, np.float32).astype(ml_dtypes.bfloat16).astype(np.float64), axis, -1)
    blocks = v.reshape(v.shape[:-1] + (-1, 32))
    amax = np.abs(blocks).max(-1, keepdims=True)
    byte = np.maximum(np.where(amax > 0, np.frexp(amax)[1] - 1 + 127, 0) - down, 1)
    scale = np.exp2(byte - 127.0)
    codes = (blocks / scale).astype(np.float32).astype(dtype).astype(np.float64)
    return np.moveaxis((codes * scale).reshape(v.shape), -1, axis)


WIDE = False


def mx_kscale(k):
    if not WIDE:
        return np.ones(k)
    levels = np.array([30, -30])
    if k % 512:
        return np.exp2(np.random.permutation(np.resize(levels, k // 32))).repeat(32)
    a = np.empty((k // 512, 16))
    for p in range(k // 512):
        a[p, :8] = np.random.permutation(np.resize(levels, 8))
        for g in range(8):
            far = levels[np.abs(levels - a[p, g]) >= 10]
            a[p, g + 8] = far[np.random.randint(len(far))]
    return np.exp2(a.ravel()).repeat(32)


def f64(x):
    return np.asarray(x).astype(np.float64)


def striped(idx):
    return np.tile(np.asarray(idx).reshape(-1, 16).T, (8, 1)).astype(np.uint16)


def unstriped(offs):
    return offs[:16].T.reshape(-1).astype(np.int64)


def striped8(idx):
    return np.asarray(idx).reshape(8, -1, 16).transpose(0, 2, 1).reshape(128, -1).astype(np.uint16)


def unstriped8(offs):
    return offs.reshape(8, 16, -1).transpose(0, 2, 1).reshape(8, -1).astype(np.int64)


def pick8(x, idx, run):
    r = np.arange(len(x))
    return x[r[:, None], idx[r % (8 * run) // run]]


E2M1 = np.array([0.0, 0.5, 1.0, 1.5, 2.0, 3.0, 4.0, 6.0, -0.0, -0.5, -1.0, -1.5, -2.0, -3.0, -4.0, -6.0])


def pack_weight(w, fmt):
    k, n = w.shape
    w = f64(np.asarray(w, np.float32).astype(ml_dtypes.bfloat16)).reshape(k // 32, 32, n)
    amax = np.abs(w).max(1)
    if fmt in ("e4m3", "e5m2"):
        byte = np.frexp(amax)[1] - 1 + 127 - (7 if fmt == "e4m3" else 14)
    else:
        mant, ex = np.frexp(amax / 6.0)
        byte = np.where(mant > 0.5, ex, ex - 1) + 127
    byte = np.clip(np.where(amax > 0, byte, 1), 1, 254)
    scaled = (w * np.exp2(127.0 - byte)[:, None, :]).reshape(k, n).astype(np.float32)
    by_word = np.ascontiguousarray(scaled.reshape(k // 512, 128, 4, n).transpose(0, 1, 3, 2))
    if fmt in ("e4m3", "e5m2"):
        words = by_word.astype(ml_dtypes.float8_e4m3fn if fmt == "e4m3" else ml_dtypes.float8_e5m2).view(np.uint8)
    else:
        c = by_word.astype(ml_dtypes.float4_e2m1fn).view(np.uint8) & 0xF
        words = (c[..., 0::2] | (c[..., 1::2] << 4)).reshape(k // 512, 128, 2 * n)
    return np.ascontiguousarray(words), np.ascontiguousarray(byte.astype(np.uint8).reshape(k // 512, 16, n))


def unpack_weight(words, scales, fmt):
    g, _, n = scales.shape
    words = np.ascontiguousarray(words).reshape(g, 128, n, -1)
    if fmt in ("e4m3", "e5m2"):
        vals = words.view(ml_dtypes.float8_e4m3fn if fmt == "e4m3" else ml_dtypes.float8_e5m2).astype(np.float64)
    else:
        nib = np.empty((g, 128, n, 4), np.uint8)
        nib[..., 0::2] = words & 0xF
        nib[..., 1::2] = words >> 4
        vals = E2M1[nib]
    vals = vals * np.repeat(np.exp2(scales.astype(np.float64) - 127.0), 8, axis=1)[..., None]
    return vals.transpose(0, 1, 3, 2).reshape(g * 512, n)


def sgn(shape):
    return np.random.uniform(0.5, 2.0, shape) * np.where(np.random.standard_normal(shape) < 0, -1.0, 1.0)


K, T, J, R, F, Z, C, O, N, S, E = 512, 1024, 256, 512, 512, 1024, 1024, 256, 256, 1024, 512


def setup_inputs():
    n = np.random.standard_normal
    idx = np.random.permutation(T)[:J]
    idx2 = np.random.permutation(Z)[:J]
    idx3 = np.random.permutation(J)[:J]
    idx4 = np.stack([np.random.permutation(C)[:J] for _ in range(8)])
    idx5 = np.stack([np.random.permutation(C)[:O] for _ in range(8)])
    idx6 = np.random.permutation(S)[:N]
    idx7 = np.stack([np.random.permutation(E)[:O] for _ in range(8)])
    fk = mx_kscale(K)
    ff = mx_kscale(F)
    fr = mx_kscale(R)
    xtp = pack_weight(n((K, T)) / fk[:, None], "e2m1")
    xop = pack_weight(n((F, Z)) / ff[:, None], "e5m2")
    wp = pack_weight(n((K, R)) * 1 / np.sqrt(K) * fk[:, None] * fr, "e5m2")
    w0p = pack_weight(n((F, R)) * 1 / np.sqrt(F) * ff[:, None] * fr, "e4m3")
    w2p = pack_weight(n((F, R)) * 1 / np.sqrt(F) * ff[:, None] * fr, "e4m3")
    vsp = pack_weight(n((R, S)) * 1 / np.sqrt(R) / fr[:, None], "e4m3")
    return {
        "xt_words": xtp[0],
        "xt_scales": xtp[1],
        "xo_words": xop[0],
        "xo_scales": xop[1],
        "w_words": wp[0],
        "w_scales": wp[1],
        "w0_words": w0p[0],
        "w0_scales": w0p[1],
        "w2_words": w2p[0],
        "w2_scales": w2p[1],
        "sa": (sgn((R, 1))).astype(np.float32),
        "vs_words": vsp[0],
        "vs_scales": vsp[1],
        "offs": striped(idx),
        "offs2": striped(idx2),
        "offs3": striped(idx3),
        "offs4": striped8(idx4),
        "offs5": striped8(idx5),
        "offs6": striped(idx6),
        "offs7": striped8(idx7),
    }


def reference(xt_words, xt_scales, xo_words, xo_scales, w_words, w_scales, w0_words, w0_scales, w2_words, w2_scales, sa, vs_words, vs_scales, offs, offs2, offs3, offs4, offs5, offs6, offs7):
    idx = unstriped(offs)
    idx2 = unstriped(offs2)
    idx3 = unstriped(offs3)
    idx4 = unstriped8(offs4)
    idx5 = unstriped8(offs5)
    idx6 = unstriped(offs6)
    idx7 = unstriped8(offs7)
    xtu = unpack_weight(xt_words, xt_scales, "e2m1")
    xou = unpack_weight(xo_words, xo_scales, "e5m2")
    wu = unpack_weight(w_words, w_scales, "e5m2")
    w0u = unpack_weight(w0_words, w0_scales, "e4m3")
    w2u = unpack_weight(w2_words, w2_scales, "e4m3")
    vsu = unpack_weight(vs_words, vs_scales, "e4m3")
    xtidxg = xtu[:, idx]
    xoidx2g = xou[:, idx2]
    a = wu.T @ xtidxg + w0u.T @ xoidx2g
    b = w2u.T @ xoidx2g
    h1 = np.maximum(a, b[:, idx3] * f64(sa))
    pw = np.zeros((R, C))
    pw[np.arange(R)[:, None], idx4[np.arange(R) % 512 // 64]] = h1
    hid = pick8(pw, idx5, 64)
    vsidx6g = vsu[:, idx6]
    hidq = mxq(hid, 0, "e5m2")
    p = vsidx6g.T @ hidq
    y = np.zeros((N, E))
    y[np.arange(N)[:, None], idx7[np.arange(N) % 128 // 16]] = p
    return y

@@ -1,0 +1,180 @@
+from contextlib import ExitStack
+
+import concourse.mybir as mybir
+
+F32 = mybir.dt.float32
+BF16 = mybir.dt.bfloat16
+I32 = mybir.dt.int32
+U32 = mybir.dt.uint32
+U16 = mybir.dt.uint16
+U8 = mybir.dt.uint8
+E4M3 = mybir.dt.float8_e4m3fn_x4
+E5M2 = mybir.dt.float8_e5m2_x4
+E2M1 = mybir.dt.float4_e2m1fn_x4
+COPY = mybir.ActivationFunctionType.Copy
+MAX = mybir.AluOpType.max
+
+P = 128
+PACK = 4
+TABLE = 1024
+HID = 512
+SLOTS = 256
+BOARD = 1024
+PAGE = 512
+WIDE = 512
+FLOPS = 469762048
+
+
+def tile_list_ownlater_noted_store_ownpage_kernel(
+    tc, xt_words, xt_scales, xo_words, xo_scales, w_words, w_scales, w0_words, w0_scales,
+    w2_words, w2_scales, sa, vs_words, vs_scales, offs, offs2, offs3, offs4, offs5, offs6, offs7, out,
+):
+    nc = tc.nc
+    with ExitStack() as ctx:
+        lists = ctx.enter_context(tc.tile_pool(name="lists", bufs=1))
+        keep = ctx.enter_context(tc.tile_pool(name="keep", bufs=1))
+        psum = ctx.enter_context(tc.psum_pool(name="psum", bufs=1))
+
+        def sbuf(name, cols, dtype, tag=None):
+            return keep.tile([P, cols], dtype, name=name, tag=tag or name, align_bytes=64)
+
+        def load_list(name, src):
+            tile = lists.tile([P, SLOTS // 16], U16, name=name)
+            nc.sync.dma_start(tile[:], src)
+            return tile
+
+        def load_words(name, src, cols):
+            tile = sbuf(name, cols, I32)
+            nc.sync.dma_start(tile[:], src[0].rearrange("p n t -> p (n t)").bitcast(I32))
+            return tile
+
+        def zero_plane(name, cols):
+            tile = sbuf(name, cols, U8)
+            nc.vector.memset(tile[:].bitcast(I32), 0)
+            return tile
+
+        def load_plane(tile, src):
+            rows = src[0].bitcast(I32)
+            for q in range(4):
+                nc.sync.dma_start(tile[32 * q : 32 * q + 4, :].bitcast(I32), rows[4 * q : 4 * q + 4, :])
+
+        def gather(name, window, offsets, dtype):
+            tile = sbuf(name, SLOTS, dtype)
+            nc.vector.tensor_copy(tile[:], window.indirect(offsets[:]))
+            return tile
+
+        def deal(name, src, dtype):
+            tile = sbuf(name, HID, dtype)
+            nc.vector.tensor_copy(
+                tile[:].rearrange("p (t m) -> p m t", t=PACK), src.rearrange("p (m t) -> p m t", t=PACK)
+            )
+            return tile
+
+        xo_plane = zero_plane("xo_plane", TABLE)
+        xt_plane = zero_plane("xt_plane", TABLE)
+        wt_plane = zero_plane("wt_plane", 3 * HID)
+        vs_plane = zero_plane("vs_plane", TABLE)
+
+        wt_rows = keep.tile([4, 4, 3, HID // 4], I32, name="wt_rows", align_bytes=64)
+        for i, src in enumerate((w2_scales, w_scales, w0_scales)):
+            nc.sync.dma_start(wt_rows[:, :, i, :], src[0].bitcast(I32).rearrange("(q r) n -> r q n", r=4))
+        xo_all = load_words("xo_all", xo_words, TABLE)
+        idx2 = load_list("idx2", offs2)
+        load_plane(xo_plane, xo_scales)
+        w2_raw = load_words("w2_raw", w2_words, HID)
+        xt_all = sbuf("xt_all", TABLE, U16)
+        nc.sync.dma_start(xt_all[:].bitcast(I32), xt_words[0].bitcast(I32))
+        idx = load_list("idx", offs)
+        idx3 = load_list("idx3", offs3)
+        sa_t = sbuf("sa_t", PACK, F32)
+        nc.gpsimd.dma_start(sa_t[:], sa.rearrange("(p t) o -> p (t o)", t=PACK))
+        w_raw = load_words("w_raw", w_words, HID)
+        w0_raw = load_words("w0_raw", w0_words, HID)
+        load_plane(xt_plane, xt_scales)
+        idx4 = load_list("idx4", offs4)
+        idx5 = load_list("idx5", offs5)
+        vs_all = load_words("vs_all", vs_words, TABLE)
+        idx6 = load_list("idx6", offs6)
+        load_plane(vs_plane, vs_scales)
+        idx7 = load_list("idx7", offs7)
+
+        for q in range(4):
+            nc.vector.tensor_copy(
+                wt_plane[32 * q : 32 * q + 4, :].bitcast(I32), wt_rows[:, q, :, :].rearrange("r i n -> r (i n)")
+            )
+        w2_s = deal("w2_s", wt_plane[:, 0:HID], U8)
+        xo_c = gather("xo_c", xo_all[:].bitcast(U32), idx2, U32)
+        xo_s = gather("xo_s", xo_plane[:], idx2, U8)
+        w2_c = deal("w2_c", w2_raw[:], I32)
+
+        def cols(t):
+            return slice(P * t, P * (t + 1))
+
+        picked = []
+        for t in range(PACK):
+            b_ps = psum.tile([P, SLOTS], F32, name="b_ps%d" % t)
+            nc.tensor.matmul_mx(
+                out=b_ps[:], lhsT=w2_c[:, cols(t)].bitcast(E4M3), lhsT_scale=w2_s[:, cols(t)],
+                rhs=xo_c[:].bitcast(E5M2), rhs_scale=xo_s[:], start=True, stop=True,
+            )
+            b_sb = sbuf("b_sb%d" % t, WIDE, F32)
+            nc.scalar.activation(b_sb[:, 0:SLOTS], b_ps[:], COPY)
+            partner = sbuf("partner%d" % t, SLOTS, F32)
+            nc.scalar.activation(partner[:], b_sb[:].indirect(idx3[:]), COPY, scale=sa_t[:, t : t + 1])
+            picked.append(partner)
+
+        w_s = deal("w_s", wt_plane[:, HID : 2 * HID], U8)
+        w0_s = deal("w0_s", wt_plane[:, 2 * HID : 3 * HID], U8)
+        xt_c = gather("xt_c", xt_all[:], idx, U16)
+        w_c = deal("w_c", w_raw[:], I32)
+        w0_c = deal("w0_c", w0_raw[:], I32)
+        xt_s = gather("xt_s", xt_plane[:], idx, U8)
+
+        boards = []
+        for t in range(PACK):
+            a_ps = psum.tile([P, SLOTS], F32, name="a_ps%d" % t)
+            nc.tensor.matmul_mx(
+                out=a_ps[:], lhsT=w_c[:, cols(t)].bitcast(E5M2), lhsT_scale=w_s[:, cols(t)],
+                rhs=xt_c[:].bitcast(E2M1), rhs_scale=xt_s[:], start=True, stop=False,
+            )
+            nc.tensor.matmul_mx(
+                out=a_ps[:], lhsT=w0_c[:, cols(t)].bitcast(E4M3), lhsT_scale=w0_s[:, cols(t)],
+                rhs=xo_c[:].bitcast(E5M2), rhs_scale=xo_s[:], start=False, stop=True,
+            )
+            kept = sbuf("kept%d" % t, SLOTS, F32)
+            nc.vector.tensor_tensor(kept[:], a_ps[:], picked[t][:], MAX)
+            board = sbuf("board%d" % t, BOARD, F32, tag=(None, None, "w_raw", "w0_raw")[t])
+            nc.vector.memset(board[:].bitcast(I32), 0)
+            nc.scalar.activation(board[:].indirect(idx4[:]), kept[:], COPY)
+            boards.append(board)
+
+        vs_s = gather("vs_s", vs_plane[:], idx6, U8)
+        vs_c = gather("vs_c", vs_all[:].bitcast(U32), idx6, U32)
+        pages = []
+        for nb in range(2):
+            page = sbuf("page%d" % nb, PAGE, F32, tag="partner%d" % nb)
+            nc.vector.memset(page[:].bitcast(I32), 0)
+            pages.append(page)
+
+        hid = keep.tile([P, PACK, SLOTS], F32, name="hid", align_bytes=64)
+        for t in range(PACK):
+            nc.vector.tensor_copy(hid[:, t, :], boards[t][:].indirect(idx5[:]))
+        hid_bf = keep.tile([P, SLOTS, PACK], BF16, name="hid_bf", align_bytes=64)
+        nc.vector.tensor_copy(
+            hid_bf[:].rearrange("p (c i) t -> p c t i", i=4), hid[:].rearrange("p t (c i) -> p c t i", i=4)
+        )
+        hid_c = sbuf("hid_c", SLOTS, U32)
+        hid_s = sbuf("hid_s", SLOTS, U8)
+        nc.vector.quantize_mx(
+            out=hid_c[:].bitcast(E5M2), scales=hid_s[:], in_=hid_bf[:].rearrange("p o t -> p (o t)")
+        )
+        for nb in range(2):
+            p_ps = psum.tile([P, SLOTS], F32, name="b_ps%d" % nb)
+            nc.tensor.matmul_mx(
+                out=p_ps[:], lhsT=vs_c[:, cols(nb)].bitcast(E4M3), lhsT_scale=vs_s[:, cols(nb)],
+                rhs=hid_c[:].bitcast(E5M2), rhs_scale=hid_s[:], start=True, stop=True,
+            )
+            p_sb = sbuf("p_sb%d" % nb, SLOTS, F32)
+            nc.vector.tensor_copy(p_sb[:], p_ps[:])
+            nc.scalar.activation(pages[nb][:].indirect(idx7[:]), p_sb[:], COPY)
+            nc.sync.dma_start(out[cols(nb), :], pages[nb][:])

@@ -53,128 +53,154 @@ def tile_list_ownlater_noted_store_ownpage_kernel(
             nc.vector.memset(tile[:].bitcast(I32), 0)
             return tile
 
-        def load_plane(tile, src):
+        def load_plane(tile, src, quadrants, queue=nc.sync):
             rows = src[0].bitcast(I32)
-            for q in range(4):
-                nc.sync.dma_start(tile[32 * q : 32 * q + 4, :].bitcast(I32), rows[4 * q : 4 * q + 4, :])
+            for q in quadrants:
+                queue.dma_start(tile[32 * q : 32 * q + 4, :].bitcast(I32), rows[4 * q : 4 * q + 4, :])
 
-        def gather(name, window, offsets, dtype):
-            tile = sbuf(name, SLOTS, dtype)
+        def gather(name, window, offsets, dtype, tag=None):
+            tile = sbuf(name, SLOTS, dtype, tag)
             nc.vector.tensor_copy(tile[:], window.indirect(offsets[:]))
             return tile
 
-        def deal(name, src, dtype):
-            tile = sbuf(name, HID, dtype)
-            nc.vector.tensor_copy(
-                tile[:].rearrange("p (t m) -> p m t", t=PACK), src.rearrange("p (m t) -> p m t", t=PACK)
-            )
-            return tile
-
         xo_plane = zero_plane("xo_plane", TABLE)
-        xt_plane = zero_plane("xt_plane", TABLE)
         wt_plane = zero_plane("wt_plane", 3 * HID)
+        xt_plane = zero_plane("xt_plane", TABLE)
         vs_plane = zero_plane("vs_plane", TABLE)
 
         wt_rows = keep.tile([4, 4, 3, HID // 4], I32, name="wt_rows", align_bytes=64)
         for i, src in enumerate((w2_scales, w_scales, w0_scales)):
             nc.sync.dma_start(wt_rows[:, :, i, :], src[0].bitcast(I32).rearrange("(q r) n -> r q n", r=4))
-        xo_all = load_words("xo_all", xo_words, TABLE)
         idx2 = load_list("idx2", offs2)
-        load_plane(xo_plane, xo_scales)
+        xo_all = load_words("xo_all", xo_words, TABLE)
         w2_raw = load_words("w2_raw", w2_words, HID)
-        xt_all = sbuf("xt_all", TABLE, U16)
-        nc.sync.dma_start(xt_all[:].bitcast(I32), xt_words[0].bitcast(I32))
+        load_plane(xo_plane, xo_scales, (0, 1, 2, 3))
         idx = load_list("idx", offs)
         idx3 = load_list("idx3", offs3)
+        w0_raw = load_words("w0_raw", w0_words, HID)
+        w_raw = load_words("w_raw", w_words, HID)
+        xt_all = sbuf("xt_all", TABLE, U16)
+        nc.sync.dma_start(xt_all[:].bitcast(I32), xt_words[0].bitcast(I32))
         sa_t = sbuf("sa_t", PACK, F32)
         nc.gpsimd.dma_start(sa_t[:], sa.rearrange("(p t) o -> p (t o)", t=PACK))
-        w_raw = load_words("w_raw", w_words, HID)
-        w0_raw = load_words("w0_raw", w0_words, HID)
-        load_plane(xt_plane, xt_scales)
+        load_plane(xt_plane, xt_scales, (0, 1, 2, 3))
         idx4 = load_list("idx4", offs4)
         idx5 = load_list("idx5", offs5)
         vs_all = load_words("vs_all", vs_words, TABLE)
         idx6 = load_list("idx6", offs6)
-        load_plane(vs_plane, vs_scales)
+        load_plane(vs_plane, vs_scales, (0, 1, 2, 3))
         idx7 = load_list("idx7", offs7)
 
         for q in range(4):
             nc.vector.tensor_copy(
                 wt_plane[32 * q : 32 * q + 4, :].bitcast(I32), wt_rows[:, q, :, :].rearrange("r i n -> r (i n)")
             )
-        w2_s = deal("w2_s", wt_plane[:, 0:HID], U8)
-        xo_c = gather("xo_c", xo_all[:].bitcast(U32), idx2, U32)
-        xo_s = gather("xo_s", xo_plane[:], idx2, U8)
-        w2_c = deal("w2_c", w2_raw[:], I32)
 
         def cols(t):
             return slice(P * t, P * (t + 1))
 
-        picked = []
-        for t in range(PACK):
+        def deal(copy, name, src, first, count, dtype, tag=None):
+            n = src.shape[1] // HID
+            tile = sbuf(name, n * count * P, dtype, tag)
+            copy(
+                tile[:].rearrange("p (w t m) -> p w m t", w=n, t=count),
+                src.rearrange("p (w m t) -> p w m t", w=n, t=PACK)[:, :, :, first : first + count],
+            )
+            return tile
+
+        on_vector, on_scalar = nc.vector.tensor_copy, nc.scalar.copy
+        picked = {}
+        boards = {}
+
+        def second_product(t):
             b_ps = psum.tile([P, SLOTS], F32, name="b_ps%d" % t)
             nc.tensor.matmul_mx(
                 out=b_ps[:], lhsT=w2_c[:, cols(t)].bitcast(E4M3), lhsT_scale=w2_s[:, cols(t)],
                 rhs=xo_c[:].bitcast(E5M2), rhs_scale=xo_s[:], start=True, stop=True,
             )
+            return b_ps
+
+        def fetch_partner(t, copy):
             b_sb = sbuf("b_sb%d" % t, WIDE, F32)
-            nc.scalar.activation(b_sb[:, 0:SLOTS], b_ps[:], COPY)
-            partner = sbuf("partner%d" % t, SLOTS, F32)
-            nc.scalar.activation(partner[:], b_sb[:].indirect(idx3[:]), COPY, scale=sa_t[:, t : t + 1])
-            picked.append(partner)
+            copy(b_sb[:, 0:SLOTS], b_banks[t][:])
+            picked[t] = sbuf("partner%d" % t, SLOTS, F32)
+            nc.scalar.activation(picked[t][:], b_sb[:].indirect(idx3[:]), COPY, scale=sa_t[:, t : t + 1])
 
-        w_s = deal("w_s", wt_plane[:, HID : 2 * HID], U8)
-        w0_s = deal("w0_s", wt_plane[:, 2 * HID : 3 * HID], U8)
+        def first_result(half, w_c, w0_c, both_s):
+            for t in (2 * half, 2 * half + 1):
+                a_ps = psum.tile([P, SLOTS], F32, name="a_ps%d" % t)
+                nc.tensor.matmul_mx(
+                    out=a_ps[:], lhsT=w0_c[:, cols(t % 2)].bitcast(E4M3), lhsT_scale=both_s[:, cols(2 + t % 2)],
+                    rhs=xo_c[:].bitcast(E5M2), rhs_scale=xo_s[:], start=True, stop=False,
+                )
+                nc.tensor.matmul_mx(
+                    out=a_ps[:], lhsT=w_c[:, cols(t % 2)].bitcast(E5M2), lhsT_scale=both_s[:, cols(t % 2)],
+                    rhs=xt_c[:].bitcast(E2M1), rhs_scale=xt_s[:], start=False, stop=True,
+                )
+                kept = sbuf("kept%d" % t, SLOTS, F32)
+                nc.vector.tensor_tensor(kept[:], a_ps[:], picked[t][:], MAX)
+                boards[t] = sbuf("board%d" % t, BOARD, F32, tag=(None, None, "xt_all", "b_sb1")[t])
+                (nc.vector if t < 2 else nc.gpsimd).memset(boards[t][:].bitcast(I32), 0)
+                nc.scalar.activation(boards[t][:].indirect(idx4[:]), kept[:], COPY)
+
+        w2_s = deal(on_vector, "w2_s", wt_plane[:, 0:HID], 0, 4, U8)
+        xo_c = gather("xo_c", xo_all[:].bitcast(U32), idx2, U32)
+        xo_s = gather("xo_s", xo_plane[:], idx2, U8)
+        w2_c = deal(on_scalar, "w2_c", w2_raw[:].bitcast(U32), 0, 4, U32)
+        w0_c = deal(on_scalar, "w0_c0", w0_raw[:].bitcast(U32), 0, 2, U32)
+        w_c = deal(on_scalar, "w_c0", w_raw[:].bitcast(U32), 0, 2, U32)
+        b_banks = [second_product(t) for t in range(PACK)]
+        fetch_partner(0, on_scalar)
+        fetch_partner(1, on_scalar)
+        both_s = deal(on_vector, "both_s0", wt_plane[:, HID : 3 * HID], 0, 2, U8)
         xt_c = gather("xt_c", xt_all[:], idx, U16)
-        w_c = deal("w_c", w_raw[:], I32)
-        w0_c = deal("w0_c", w0_raw[:], I32)
         xt_s = gather("xt_s", xt_plane[:], idx, U8)
+        fetch_partner(2, on_vector)
+        fetch_partner(3, on_vector)
+        first_result(0, w_c, w0_c, both_s)
 
-        boards = []
-        for t in range(PACK):
-            a_ps = psum.tile([P, SLOTS], F32, name="a_ps%d" % t)
-            nc.tensor.matmul_mx(
-                out=a_ps[:], lhsT=w_c[:, cols(t)].bitcast(E5M2), lhsT_scale=w_s[:, cols(t)],
-                rhs=xt_c[:].bitcast(E2M1), rhs_scale=xt_s[:], start=True, stop=False,
-            )
-            nc.tensor.matmul_mx(
-                out=a_ps[:], lhsT=w0_c[:, cols(t)].bitcast(E4M3), lhsT_scale=w0_s[:, cols(t)],
-                rhs=xo_c[:].bitcast(E5M2), rhs_scale=xo_s[:], start=False, stop=True,
-            )
-            kept = sbuf("kept%d" % t, SLOTS, F32)
-            nc.vector.tensor_tensor(kept[:], a_ps[:], picked[t][:], MAX)
-            board = sbuf("board%d" % t, BOARD, F32, tag=(None, None, "w_raw", "w0_raw")[t])
-            nc.vector.memset(board[:].bitcast(I32), 0)
-            nc.scalar.activation(board[:].indirect(idx4[:]), kept[:], COPY)
-            boards.append(board)
+        both_s = deal(on_vector, "both_s1", wt_plane[:, HID : 3 * HID], 2, 2, U8, "partner0")
+        w0_c = deal(on_vector, "w0_c1", w0_raw[:], 2, 2, I32, "xt_plane")
+        w_c = deal(on_vector, "w_c1", w_raw[:], 2, 2, I32, "partner1")
+        first_result(1, w_c, w0_c, both_s)
 
-        vs_s = gather("vs_s", vs_plane[:], idx6, U8)
-        vs_c = gather("vs_c", vs_all[:].bitcast(U32), idx6, U32)
+        vs_s = gather("vs_s", vs_plane[:], idx6, U8, "partner2")
+        vs_c = gather("vs_c", vs_all[:].bitcast(U32), idx6, U32, "vs_plane")
         pages = []
         for nb in range(2):
-            page = sbuf("page%d" % nb, PAGE, F32, tag="partner%d" % nb)
-            nc.vector.memset(page[:].bitcast(I32), 0)
+            page = sbuf("page%d" % nb, PAGE, F32, tag="kept%d" % nb)
+            nc.gpsimd.memset(page[:].bitcast(I32), 0)
             pages.append(page)
 
-        hid = keep.tile([P, PACK, SLOTS], F32, name="hid", align_bytes=64)
+        hid = keep.tile([P, PACK, SLOTS], F32, name="hid", tag="vs_all", align_bytes=64)
+        halves = [keep.tile([P, P, PACK], BF16, name="hid_bf%d" % h, align_bytes=64) for h in range(2)]
         for t in range(PACK):
             nc.vector.tensor_copy(hid[:, t, :], boards[t][:].indirect(idx5[:]))
-        hid_bf = keep.tile([P, SLOTS, PACK], BF16, name="hid_bf", align_bytes=64)
-        nc.vector.tensor_copy(
-            hid_bf[:].rearrange("p (c i) t -> p c t i", i=4), hid[:].rearrange("p t (c i) -> p c t i", i=4)
-        )
-        hid_c = sbuf("hid_c", SLOTS, U32)
-        hid_s = sbuf("hid_s", SLOTS, U8)
-        nc.vector.quantize_mx(
-            out=hid_c[:].bitcast(E5M2), scales=hid_s[:], in_=hid_bf[:].rearrange("p o t -> p (o t)")
-        )
-        for nb in range(2):
-            p_ps = psum.tile([P, SLOTS], F32, name="b_ps%d" % nb)
-            nc.tensor.matmul_mx(
-                out=p_ps[:], lhsT=vs_c[:, cols(nb)].bitcast(E4M3), lhsT_scale=vs_s[:, cols(nb)],
-                rhs=hid_c[:].bitcast(E5M2), rhs_scale=hid_s[:], start=True, stop=True,
+            if t == 2:
+                for h in range(2):
+                    nc.vector.tensor_copy(
+                        halves[h][:, :, 0:3], hid[:, 0:3, cols(h)].rearrange("p t o -> p o t")
+                    )
+        for h in range(2):
+            nc.vector.tensor_copy(halves[h][:, :, 3], hid[:, 3, cols(h)])
+        codes = []
+        for h in range(2):
+            hid_c = sbuf("hid_c%d" % h, P, U32)
+            hid_s = sbuf("hid_s%d" % h, P, U8)
+            nc.vector.quantize_mx(
+                out=hid_c[:].bitcast(E5M2), scales=hid_s[:], in_=halves[h][:].rearrange("p o t -> p (o t)")
             )
-            p_sb = sbuf("p_sb%d" % nb, SLOTS, F32)
-            nc.vector.tensor_copy(p_sb[:], p_ps[:])
-            nc.scalar.activation(pages[nb][:].indirect(idx7[:]), p_sb[:], COPY)
+            codes.append((hid_c, hid_s))
+        for h in range(2):
+            hid_c, hid_s = codes[h]
+            for nb in range(2):
+                p_ps = psum.tile([P, P], F32, name="b_ps%d" % (2 * h + nb))
+                nc.tensor.matmul_mx(
+                    out=p_ps[:], lhsT=vs_c[:, cols(nb)].bitcast(E4M3), lhsT_scale=vs_s[:, cols(nb)],
+                    rhs=hid_c[:].bitcast(E5M2), rhs_scale=hid_s[:], start=True, stop=True,
+                )
+                p_sb = sbuf("p_sb%d" % (2 * h + nb), P, F32)
+                nc.vector.tensor_copy(p_sb[:], p_ps[:])
+                nc.scalar.activation(pages[nb][:].indirect(idx7[:, 8 * h : 8 * h + 8]), p_sb[:], COPY)
+        for nb in range(2):
             nc.sync.dma_start(out[cols(nb), :], pages[nb][:])

@@ -75,10 +75,10 @@ def tile_list_ownlater_noted_store_ownpage_kernel(
         xo_all = load_words("xo_all", xo_words, TABLE)
         w2_raw = load_words("w2_raw", w2_words, HID)
         load_plane(xo_plane, xo_scales, (0, 1, 2, 3))
-        idx = load_list("idx", offs)
-        idx3 = load_list("idx3", offs3)
         w0_raw = load_words("w0_raw", w0_words, HID)
         w_raw = load_words("w_raw", w_words, HID)
+        idx = load_list("idx", offs)
+        idx3 = load_list("idx3", offs3)
         xt_all = sbuf("xt_all", TABLE, U16)
         nc.sync.dma_start(xt_all[:].bitcast(I32), xt_words[0].bitcast(I32))
         sa_t = sbuf("sa_t", PACK, F32)
@@ -102,14 +102,14 @@ def tile_list_ownlater_noted_store_ownpage_kernel(
         def deal(copy, name, src, first, count, dtype, tag=None):
             n = src.shape[1] // HID
             tile = sbuf(name, n * count * P, dtype, tag)
+            run = 16 if dtype == U8 else 4
             copy(
-                tile[:].rearrange("p (w t m) -> p w m t", w=n, t=count),
-                src.rearrange("p (w m t) -> p w m t", w=n, t=PACK)[:, :, :, first : first + count],
+                tile[:].rearrange("p (w t c i) -> p w c t i", w=n, t=count, i=run),
+                src.rearrange("p (w c i t) -> p w c t i", w=n, i=run, t=PACK)[:, :, :, first : first + count, :],
             )
             return tile
 
         on_vector, on_scalar = nc.vector.tensor_copy, nc.scalar.copy
-        picked = {}
         boards = {}
 
         def second_product(t):
@@ -123,23 +123,22 @@ def tile_list_ownlater_noted_store_ownpage_kernel(
         def fetch_partner(t, copy):
             b_sb = sbuf("b_sb%d" % t, WIDE, F32)
             copy(b_sb[:, 0:SLOTS], b_banks[t][:])
-            picked[t] = sbuf("partner%d" % t, SLOTS, F32)
-            nc.scalar.activation(picked[t][:], b_sb[:].indirect(idx3[:]), COPY, scale=sa_t[:, t : t + 1])
+            nc.scalar.activation(picked[t], b_sb[:].indirect(idx3[:]), COPY, scale=sa_t[:, t : t + 1])
 
         def first_result(half, w_c, w0_c, both_s):
             for t in (2 * half, 2 * half + 1):
                 a_ps = psum.tile([P, SLOTS], F32, name="a_ps%d" % t)
                 nc.tensor.matmul_mx(
-                    out=a_ps[:], lhsT=w0_c[:, cols(t % 2)].bitcast(E4M3), lhsT_scale=both_s[:, cols(2 + t % 2)],
+                    out=a_ps[:], lhsT=w0_c[:, cols(t)].bitcast(E4M3), lhsT_scale=both_s[:, cols(2 + t % 2)],
                     rhs=xo_c[:].bitcast(E5M2), rhs_scale=xo_s[:], start=True, stop=False,
                 )
                 nc.tensor.matmul_mx(
-                    out=a_ps[:], lhsT=w_c[:, cols(t % 2)].bitcast(E5M2), lhsT_scale=both_s[:, cols(t % 2)],
+                    out=a_ps[:], lhsT=w_c[:, cols(t)].bitcast(E5M2), lhsT_scale=both_s[:, cols(t % 2)],
                     rhs=xt_c[:].bitcast(E2M1), rhs_scale=xt_s[:], start=False, stop=True,
                 )
                 kept = sbuf("kept%d" % t, SLOTS, F32)
-                nc.vector.tensor_tensor(kept[:], a_ps[:], picked[t][:], MAX)
-                boards[t] = sbuf("board%d" % t, BOARD, F32, tag=(None, None, "xt_all", "b_sb1")[t])
+                nc.vector.tensor_tensor(kept[:], a_ps[:], picked[t], MAX)
+                boards[t] = sbuf("board%d" % t, BOARD, F32, tag=(None, None, "xt_plane", "kept0")[t])
                 (nc.vector if t < 2 else nc.gpsimd).memset(boards[t][:].bitcast(I32), 0)
                 nc.scalar.activation(boards[t][:].indirect(idx4[:]), kept[:], COPY)
 
@@ -147,28 +146,29 @@ def tile_list_ownlater_noted_store_ownpage_kernel(
         xo_c = gather("xo_c", xo_all[:].bitcast(U32), idx2, U32)
         xo_s = gather("xo_s", xo_plane[:], idx2, U8)
         w2_c = deal(on_scalar, "w2_c", w2_raw[:].bitcast(U32), 0, 4, U32)
-        w0_c = deal(on_scalar, "w0_c0", w0_raw[:].bitcast(U32), 0, 2, U32)
-        w_c = deal(on_scalar, "w_c0", w_raw[:].bitcast(U32), 0, 2, U32)
+        w0_c = deal(on_scalar, "w0_c0", w0_raw[:].bitcast(U32), 0, 4, U32)
+        w_c = deal(on_scalar, "w_c0", w_raw[:].bitcast(U32), 0, 4, U32)
+        picked_first = sbuf("picked_first", SLOTS, F32, "w_raw")
+        picked_rest = sbuf("picked_rest", 3 * SLOTS, F32, "w0_raw")
+        picked = [picked_first[:]] + [picked_rest[:, SLOTS * i : SLOTS * (i + 1)] for i in range(3)]
         b_banks = [second_product(t) for t in range(PACK)]
         fetch_partner(0, on_scalar)
         fetch_partner(1, on_scalar)
         both_s = deal(on_vector, "both_s0", wt_plane[:, HID : 3 * HID], 0, 2, U8)
-        xt_c = gather("xt_c", xt_all[:], idx, U16)
-        xt_s = gather("xt_s", xt_plane[:], idx, U8)
         fetch_partner(2, on_vector)
         fetch_partner(3, on_vector)
+        xt_c = gather("xt_c", xt_all[:], idx, U16)
+        xt_s = gather("xt_s", xt_plane[:], idx, U8)
         first_result(0, w_c, w0_c, both_s)
 
-        both_s = deal(on_vector, "both_s1", wt_plane[:, HID : 3 * HID], 2, 2, U8, "partner0")
-        w0_c = deal(on_vector, "w0_c1", w0_raw[:], 2, 2, I32, "xt_plane")
-        w_c = deal(on_vector, "w_c1", w_raw[:], 2, 2, I32, "partner1")
+        both_s = deal(on_vector, "both_s1", wt_plane[:, HID : 3 * HID], 2, 2, U8, "w_raw")
         first_result(1, w_c, w0_c, both_s)
 
-        vs_s = gather("vs_s", vs_plane[:], idx6, U8, "partner2")
+        vs_s = gather("vs_s", vs_plane[:], idx6, U8, "both_s0")
         vs_c = gather("vs_c", vs_all[:].bitcast(U32), idx6, U32, "vs_plane")
         pages = []
         for nb in range(2):
-            page = sbuf("page%d" % nb, PAGE, F32, tag="kept%d" % nb)
+            page = sbuf("page%d" % nb, PAGE, F32, tag="kept%d" % (nb + 1))
             nc.gpsimd.memset(page[:].bitcast(I32), 0)
             pages.append(page)
 

@@ -115,15 +115,24 @@ def tile_list_ownlater_noted_store_ownpage_kernel(
         def second_product(t):
             b_ps = psum.tile([P, SLOTS], F32, name="b_ps%d" % t)
             nc.tensor.matmul_mx(
-                out=b_ps[:], lhsT=w2_c[:, cols(t)].bitcast(E4M3), lhsT_scale=w2_s[:, cols(t)],
+                out=b_ps[:], lhsT=w2_c[:, cols(t)].bitcast(E4M3), lhsT_scale=w2_s[t // 2][:, cols(t % 2)],
                 rhs=xo_c[:].bitcast(E5M2), rhs_scale=xo_s[:], start=True, stop=True,
             )
             return b_ps
 
-        def fetch_partner(t, copy):
+        def fetch_partner(t):
             b_sb = sbuf("b_sb%d" % t, WIDE, F32)
-            copy(b_sb[:, 0:SLOTS], b_banks[t][:])
+            nc.scalar.copy(b_sb[:, 0:SLOTS], b_banks[t][:])
             nc.scalar.activation(picked[t], b_sb[:].indirect(idx3[:]), COPY, scale=sa_t[:, t : t + 1])
+
+        def fetch_last_partner(t):
+            b_sb = sbuf("b_sb%d" % t, SLOTS, F32, "xt_plane")
+            nc.vector.tensor_copy(b_sb[:], b_banks[t][:])
+            for h in range(2):
+                nc.scalar.activation(
+                    picked[t][:, cols(h)], b_sb[:].indirect(idx3[:, 8 * h : 8 * h + 8]), COPY,
+                    scale=sa_t[:, t : t + 1],
+                )
 
         def first_result(half, w_c, w0_c, both_s):
             for t in (2 * half, 2 * half + 1):
@@ -142,26 +151,26 @@ def tile_list_ownlater_noted_store_ownpage_kernel(
                 (nc.vector if t < 2 else nc.gpsimd).memset(boards[t][:].bitcast(I32), 0)
                 nc.scalar.activation(boards[t][:].indirect(idx4[:]), kept[:], COPY)
 
-        w2_s = deal(on_vector, "w2_s", wt_plane[:, 0:HID], 0, 4, U8)
+        w2_s = [deal(on_vector, "w2_s0", wt_plane[:, 0:HID], 0, 2, U8)]
         xo_c = gather("xo_c", xo_all[:].bitcast(U32), idx2, U32)
         xo_s = gather("xo_s", xo_plane[:], idx2, U8)
+        w2_s.append(deal(on_vector, "w2_s1", wt_plane[:, 0:HID], 2, 2, U8, "xo_plane"))
         w2_c = deal(on_scalar, "w2_c", w2_raw[:].bitcast(U32), 0, 4, U32)
         w0_c = deal(on_scalar, "w0_c0", w0_raw[:].bitcast(U32), 0, 4, U32)
-        w_c = deal(on_scalar, "w_c0", w_raw[:].bitcast(U32), 0, 4, U32)
-        picked_first = sbuf("picked_first", SLOTS, F32, "w_raw")
-        picked_rest = sbuf("picked_rest", 3 * SLOTS, F32, "w0_raw")
+        both_s = deal(on_vector, "both_s0", wt_plane[:, HID : 3 * HID], 0, 2, U8)
+        w_c = deal(on_vector, "w_c", w_raw[:], 0, 4, I32)
+        picked_first = sbuf("picked_first", SLOTS, F32, "w0_raw")
+        picked_rest = sbuf("picked_rest", 3 * SLOTS, F32, "w_raw")
         picked = [picked_first[:]] + [picked_rest[:, SLOTS * i : SLOTS * (i + 1)] for i in range(3)]
         b_banks = [second_product(t) for t in range(PACK)]
-        fetch_partner(0, on_scalar)
-        fetch_partner(1, on_scalar)
-        both_s = deal(on_vector, "both_s0", wt_plane[:, HID : 3 * HID], 0, 2, U8)
-        fetch_partner(2, on_vector)
-        fetch_partner(3, on_vector)
+        for t in range(PACK - 1):
+            fetch_partner(t)
         xt_c = gather("xt_c", xt_all[:], idx, U16)
         xt_s = gather("xt_s", xt_plane[:], idx, U8)
+        fetch_last_partner(PACK - 1)
         first_result(0, w_c, w0_c, both_s)
 
-        both_s = deal(on_vector, "both_s1", wt_plane[:, HID : 3 * HID], 2, 2, U8, "w_raw")
+        both_s = deal(on_vector, "both_s1", wt_plane[:, HID : 3 * HID], 2, 2, U8, "w0_raw")
         first_result(1, w_c, w0_c, both_s)
 
         vs_s = gather("vs_s", vs_plane[:], idx6, U8, "both_s0")

@@ -16,12 +16,15 @@ MAX = mybir.AluOpType.max
 
 P = 128
 PACK = 4
+QUADRANTS = 4
 TABLE = 1024
 HID = 512
 SLOTS = 256
 BOARD = 1024
 PAGE = 512
 WIDE = 512
+LINE = 16
+HALF = SLOTS // 16 // 2
 FLOPS = 469762048
 
 
@@ -35,31 +38,31 @@ def tile_list_ownlater_noted_store_ownpage_kernel(
         keep = ctx.enter_context(tc.tile_pool(name="keep", bufs=1))
         psum = ctx.enter_context(tc.psum_pool(name="psum", bufs=1))
 
-        def sbuf(name, cols, dtype, tag=None):
-            return keep.tile([P, cols], dtype, name=name, tag=tag or name, align_bytes=64)
+        def sbuf(name, width, dtype, after=None):
+            return keep.tile([P, width], dtype, name=name, tag=after or name, align_bytes=64)
 
         def load_list(name, src):
             tile = lists.tile([P, SLOTS // 16], U16, name=name)
             nc.sync.dma_start(tile[:], src)
             return tile
 
-        def load_words(name, src, cols):
-            tile = sbuf(name, cols, I32)
+        def load_words(name, src, width):
+            tile = sbuf(name, width, I32)
             nc.sync.dma_start(tile[:], src[0].rearrange("p n t -> p (n t)").bitcast(I32))
             return tile
 
-        def zero_plane(name, cols):
-            tile = sbuf(name, cols, U8)
+        def zero_plane(name, width):
+            tile = sbuf(name, width, U8)
             nc.vector.memset(tile[:].bitcast(I32), 0)
             return tile
 
-        def load_plane(tile, src, quadrants, queue=nc.sync):
+        def load_plane(tile, src):
             rows = src[0].bitcast(I32)
-            for q in quadrants:
-                queue.dma_start(tile[32 * q : 32 * q + 4, :].bitcast(I32), rows[4 * q : 4 * q + 4, :])
+            for q in range(QUADRANTS):
+                nc.sync.dma_start(tile[32 * q : 32 * q + 4, :].bitcast(I32), rows[4 * q : 4 * q + 4, :])
 
-        def gather(name, window, offsets, dtype, tag=None):
-            tile = sbuf(name, SLOTS, dtype, tag)
+        def gather(name, window, offsets, dtype, after=None):
+            tile = sbuf(name, SLOTS, dtype, after)
             nc.vector.tensor_copy(tile[:], window.indirect(offsets[:]))
             return tile
 
@@ -68,13 +71,13 @@ def tile_list_ownlater_noted_store_ownpage_kernel(
         xt_plane = zero_plane("xt_plane", TABLE)
         vs_plane = zero_plane("vs_plane", TABLE)
 
-        wt_rows = keep.tile([4, 4, 3, HID // 4], I32, name="wt_rows", align_bytes=64)
+        wt_rows = keep.tile([4, QUADRANTS, 3, HID // 4], I32, name="wt_rows", align_bytes=64)
         for i, src in enumerate((w2_scales, w_scales, w0_scales)):
-            nc.sync.dma_start(wt_rows[:, :, i, :], src[0].bitcast(I32).rearrange("(q r) n -> r q n", r=4))
+            nc.sync.dma_start(wt_rows[:, :, i, :], src[0].bitcast(I32).rearrange("(q s) n -> s q n", s=4))
         idx2 = load_list("idx2", offs2)
         xo_all = load_words("xo_all", xo_words, TABLE)
         w2_raw = load_words("w2_raw", w2_words, HID)
-        load_plane(xo_plane, xo_scales, (0, 1, 2, 3))
+        load_plane(xo_plane, xo_scales)
         w0_raw = load_words("w0_raw", w0_words, HID)
         w_raw = load_words("w_raw", w_words, HID)
         idx = load_list("idx", offs)
@@ -83,33 +86,35 @@ def tile_list_ownlater_noted_store_ownpage_kernel(
         nc.sync.dma_start(xt_all[:].bitcast(I32), xt_words[0].bitcast(I32))
         sa_t = sbuf("sa_t", PACK, F32)
         nc.gpsimd.dma_start(sa_t[:], sa.rearrange("(p t) o -> p (t o)", t=PACK))
-        load_plane(xt_plane, xt_scales, (0, 1, 2, 3))
+        load_plane(xt_plane, xt_scales)
         idx4 = load_list("idx4", offs4)
         idx5 = load_list("idx5", offs5)
         vs_all = load_words("vs_all", vs_words, TABLE)
         idx6 = load_list("idx6", offs6)
-        load_plane(vs_plane, vs_scales, (0, 1, 2, 3))
+        load_plane(vs_plane, vs_scales)
         idx7 = load_list("idx7", offs7)
 
-        for q in range(4):
+        for q in range(QUADRANTS):
             nc.vector.tensor_copy(
-                wt_plane[32 * q : 32 * q + 4, :].bitcast(I32), wt_rows[:, q, :, :].rearrange("r i n -> r (i n)")
+                wt_plane[32 * q : 32 * q + 4, :].bitcast(I32), wt_rows[:, q, :, :].rearrange("s i n -> s (i n)")
             )
 
-        def cols(t):
-            return slice(P * t, P * (t + 1))
+        def cols(i):
+            return slice(P * i, P * (i + 1))
 
-        def deal(copy, name, src, first, count, dtype, tag=None):
-            n = src.shape[1] // HID
-            tile = sbuf(name, n * count * P, dtype, tag)
-            run = 16 if dtype == U8 else 4
+        def half_list(offsets, h):
+            return offsets[:, HALF * h : HALF * (h + 1)]
+
+        def deal(copy, name, src, first, count, dtype, after=None):
+            weights = src.shape[1] // HID
+            tile = sbuf(name, weights * count * P, dtype, after)
+            run = LINE if dtype == U8 else LINE // 4
             copy(
-                tile[:].rearrange("p (w t c i) -> p w c t i", w=n, t=count, i=run),
-                src.rearrange("p (w c i t) -> p w c t i", w=n, i=run, t=PACK)[:, :, :, first : first + count, :],
+                tile[:].rearrange("p (w t c i) -> p w c t i", w=weights, t=count, i=run),
+                src.rearrange("p (w c i t) -> p w c t i", w=weights, i=run, t=PACK)[:, :, :, first : first + count, :],
             )
             return tile
 
-        on_vector, on_scalar = nc.vector.tensor_copy, nc.scalar.copy
         boards = {}
 
         def second_product(t):
@@ -130,68 +135,71 @@ def tile_list_ownlater_noted_store_ownpage_kernel(
             nc.vector.tensor_copy(b_sb[:], b_banks[t][:])
             for h in range(2):
                 nc.scalar.activation(
-                    picked[t][:, cols(h)], b_sb[:].indirect(idx3[:, 8 * h : 8 * h + 8]), COPY,
-                    scale=sa_t[:, t : t + 1],
+                    picked[t][:, cols(h)], b_sb[:].indirect(half_list(idx3, h)), COPY, scale=sa_t[:, t : t + 1]
                 )
 
-        def first_result(half, w_c, w0_c, both_s):
-            for t in (2 * half, 2 * half + 1):
+        board_after = (None, "xt_all", "xt_plane", "kept0")
+
+        def first_result(pair, pair_s):
+            for t in (2 * pair, 2 * pair + 1):
                 a_ps = psum.tile([P, SLOTS], F32, name="a_ps%d" % t)
                 nc.tensor.matmul_mx(
-                    out=a_ps[:], lhsT=w0_c[:, cols(t)].bitcast(E4M3), lhsT_scale=both_s[:, cols(2 + t % 2)],
+                    out=a_ps[:], lhsT=w0_c[:, cols(t)].bitcast(E4M3), lhsT_scale=pair_s[:, cols(2 + t % 2)],
                     rhs=xo_c[:].bitcast(E5M2), rhs_scale=xo_s[:], start=True, stop=False,
                 )
                 nc.tensor.matmul_mx(
-                    out=a_ps[:], lhsT=w_c[:, cols(t)].bitcast(E5M2), lhsT_scale=both_s[:, cols(t % 2)],
+                    out=a_ps[:], lhsT=w_c[:, cols(t)].bitcast(E5M2), lhsT_scale=pair_s[:, cols(t % 2)],
                     rhs=xt_c[:].bitcast(E2M1), rhs_scale=xt_s[:], start=False, stop=True,
                 )
                 kept = sbuf("kept%d" % t, SLOTS, F32)
                 nc.vector.tensor_tensor(kept[:], a_ps[:], picked[t], MAX)
-                boards[t] = sbuf("board%d" % t, BOARD, F32, tag=(None, None, "xt_plane", "kept0")[t])
-                (nc.vector if t < 2 else nc.gpsimd).memset(boards[t][:].bitcast(I32), 0)
+                boards[t] = sbuf("board%d" % t, BOARD, F32, board_after[t])
+                zeroing = nc.vector if board_after[t] is None else nc.gpsimd
+                zeroing.memset(boards[t][:].bitcast(I32), 0)
                 nc.scalar.activation(boards[t][:].indirect(idx4[:]), kept[:], COPY)
 
-        w2_s = [deal(on_vector, "w2_s0", wt_plane[:, 0:HID], 0, 2, U8)]
+        w2_s = [deal(nc.vector.tensor_copy, "w2_s0", wt_plane[:, 0:HID], 0, 2, U8)]
         xo_c = gather("xo_c", xo_all[:].bitcast(U32), idx2, U32)
         xo_s = gather("xo_s", xo_plane[:], idx2, U8)
-        w2_s.append(deal(on_vector, "w2_s1", wt_plane[:, 0:HID], 2, 2, U8, "xo_plane"))
-        w2_c = deal(on_scalar, "w2_c", w2_raw[:].bitcast(U32), 0, 4, U32)
-        w0_c = deal(on_scalar, "w0_c0", w0_raw[:].bitcast(U32), 0, 4, U32)
-        both_s = deal(on_vector, "both_s0", wt_plane[:, HID : 3 * HID], 0, 2, U8)
-        w_c = deal(on_vector, "w_c", w_raw[:], 0, 4, I32)
+        w2_s.append(deal(nc.vector.tensor_copy, "w2_s1", wt_plane[:, 0:HID], 2, 2, U8, "xo_plane"))
+        w2_c = deal(nc.scalar.copy, "w2_c", w2_raw[:].bitcast(U32), 0, PACK, U32)
+        w0_c = deal(nc.scalar.copy, "w0_c0", w0_raw[:].bitcast(U32), 0, PACK, U32)
+        lower_s = deal(nc.vector.tensor_copy, "both_s0", wt_plane[:, HID : 3 * HID], 0, 2, U8)
+        w_c = deal(nc.vector.tensor_copy, "w_c", w_raw[:], 0, PACK, I32)
+
         picked_first = sbuf("picked_first", SLOTS, F32, "w0_raw")
-        picked_rest = sbuf("picked_rest", 3 * SLOTS, F32, "w_raw")
-        picked = [picked_first[:]] + [picked_rest[:, SLOTS * i : SLOTS * (i + 1)] for i in range(3)]
+        picked_rest = sbuf("picked_rest", (PACK - 1) * SLOTS, F32, "w_raw")
+        picked = [picked_first[:]] + [picked_rest[:, SLOTS * i : SLOTS * (i + 1)] for i in range(PACK - 1)]
         b_banks = [second_product(t) for t in range(PACK)]
         for t in range(PACK - 1):
             fetch_partner(t)
         xt_c = gather("xt_c", xt_all[:], idx, U16)
         xt_s = gather("xt_s", xt_plane[:], idx, U8)
         fetch_last_partner(PACK - 1)
-        first_result(0, w_c, w0_c, both_s)
+        first_result(0, lower_s)
 
-        both_s = deal(on_vector, "both_s1", wt_plane[:, HID : 3 * HID], 2, 2, U8, "w0_raw")
-        first_result(1, w_c, w0_c, both_s)
+        upper_s = deal(nc.vector.tensor_copy, "both_s1", wt_plane[:, HID : 3 * HID], 2, 2, U8, "w0_raw")
+        first_result(1, upper_s)
 
         vs_s = gather("vs_s", vs_plane[:], idx6, U8, "both_s0")
         vs_c = gather("vs_c", vs_all[:].bitcast(U32), idx6, U32, "vs_plane")
         pages = []
         for nb in range(2):
-            page = sbuf("page%d" % nb, PAGE, F32, tag="kept%d" % (nb + 1))
+            page = sbuf("page%d" % nb, PAGE, F32, "kept%d" % (nb + 1))
             nc.gpsimd.memset(page[:].bitcast(I32), 0)
             pages.append(page)
 
+        last = PACK - 1
         hid = keep.tile([P, PACK, SLOTS], F32, name="hid", tag="vs_all", align_bytes=64)
         halves = [keep.tile([P, P, PACK], BF16, name="hid_bf%d" % h, align_bytes=64) for h in range(2)]
-        for t in range(PACK):
+        for t in range(last):
             nc.vector.tensor_copy(hid[:, t, :], boards[t][:].indirect(idx5[:]))
-            if t == 2:
-                for h in range(2):
-                    nc.vector.tensor_copy(
-                        halves[h][:, :, 0:3], hid[:, 0:3, cols(h)].rearrange("p t o -> p o t")
-                    )
         for h in range(2):
-            nc.vector.tensor_copy(halves[h][:, :, 3], hid[:, 3, cols(h)])
+            nc.vector.tensor_copy(halves[h][:, :, 0:last], hid[:, 0:last, cols(h)].rearrange("p t o -> p o t"))
+        nc.vector.tensor_copy(hid[:, last, :], boards[last][:].indirect(idx5[:]))
+        for h in range(2):
+            nc.vector.tensor_copy(halves[h][:, :, last], hid[:, last, cols(h)])
+
         codes = []
         for h in range(2):
             hid_c = sbuf("hid_c%d" % h, P, U32)
@@ -210,6 +218,6 @@ def tile_list_ownlater_noted_store_ownpage_kernel(
                 )
                 p_sb = sbuf("p_sb%d" % (2 * h + nb), P, F32)
                 nc.vector.tensor_copy(p_sb[:], p_ps[:])
-                nc.scalar.activation(pages[nb][:].indirect(idx7[:, 8 * h : 8 * h + 8]), p_sb[:], COPY)
+                nc.scalar.activation(pages[nb][:].indirect(half_list(idx7, h)), p_sb[:], COPY)
         for nb in range(2):
             nc.sync.dma_start(out[cols(nb), :], pages[nb][:])

from contextlib import ExitStack

import concourse.mybir as mybir

F32 = mybir.dt.float32
BF16 = mybir.dt.bfloat16
I32 = mybir.dt.int32
U32 = mybir.dt.uint32
U16 = mybir.dt.uint16
U8 = mybir.dt.uint8
E4M3 = mybir.dt.float8_e4m3fn_x4
E5M2 = mybir.dt.float8_e5m2_x4
E2M1 = mybir.dt.float4_e2m1fn_x4
COPY = mybir.ActivationFunctionType.Copy
MAX = mybir.AluOpType.max

P = 128
PACK = 4
QUADRANTS = 4
TABLE = 1024
HID = 512
SLOTS = 256
BOARD = 1024
PAGE = 512
WIDE = 512
LINE = 16
HALF = SLOTS // 16 // 2
FLOPS = 469762048


def tile_list_ownlater_noted_store_ownpage_kernel(
    tc, xt_words, xt_scales, xo_words, xo_scales, w_words, w_scales, w0_words, w0_scales,
    w2_words, w2_scales, sa, vs_words, vs_scales, offs, offs2, offs3, offs4, offs5, offs6, offs7, out,
):
    nc = tc.nc
    with ExitStack() as ctx:
        lists = ctx.enter_context(tc.tile_pool(name="lists", bufs=1))
        keep = ctx.enter_context(tc.tile_pool(name="keep", bufs=1))
        psum = ctx.enter_context(tc.psum_pool(name="psum", bufs=1))

        def sbuf(name, width, dtype, after=None):
            return keep.tile([P, width], dtype, name=name, tag=after or name, align_bytes=64)

        def load_list(name, src):
            tile = lists.tile([P, SLOTS // 16], U16, name=name)
            nc.sync.dma_start(tile[:], src)
            return tile

        def load_words(name, src, width):
            tile = sbuf(name, width, I32)
            nc.sync.dma_start(tile[:], src[0].rearrange("p n t -> p (n t)").bitcast(I32))
            return tile

        def zero_plane(name, width):
            tile = sbuf(name, width, U8)
            nc.vector.memset(tile[:].bitcast(I32), 0)
            return tile

        def load_plane(tile, src):
            rows = src[0].bitcast(I32)
            for q in range(QUADRANTS):
                nc.sync.dma_start(tile[32 * q : 32 * q + 4, :].bitcast(I32), rows[4 * q : 4 * q + 4, :])

        def gather(name, window, offsets, dtype, after=None):
            tile = sbuf(name, SLOTS, dtype, after)
            nc.vector.tensor_copy(tile[:], window.indirect(offsets[:]))
            return tile

        xo_plane = zero_plane("xo_plane", TABLE)
        wt_plane = zero_plane("wt_plane", 3 * HID)
        xt_plane = zero_plane("xt_plane", TABLE)
        vs_plane = zero_plane("vs_plane", TABLE)

        wt_rows = keep.tile([4, QUADRANTS, 3, HID // 4], I32, name="wt_rows", align_bytes=64)
        for i, src in enumerate((w2_scales, w_scales, w0_scales)):
            nc.sync.dma_start(wt_rows[:, :, i, :], src[0].bitcast(I32).rearrange("(q s) n -> s q n", s=4))
        idx2 = load_list("idx2", offs2)
        xo_all = load_words("xo_all", xo_words, TABLE)
        w2_raw = load_words("w2_raw", w2_words, HID)
        load_plane(xo_plane, xo_scales)
        w0_raw = load_words("w0_raw", w0_words, HID)
        w_raw = load_words("w_raw", w_words, HID)
        idx = load_list("idx", offs)
        idx3 = load_list("idx3", offs3)
        xt_all = sbuf("xt_all", TABLE, U16)
        nc.sync.dma_start(xt_all[:].bitcast(I32), xt_words[0].bitcast(I32))
        sa_t = sbuf("sa_t", PACK, F32)
        nc.gpsimd.dma_start(sa_t[:], sa.rearrange("(p t) o -> p (t o)", t=PACK))
        load_plane(xt_plane, xt_scales)
        idx4 = load_list("idx4", offs4)
        idx5 = load_list("idx5", offs5)
        vs_all = load_words("vs_all", vs_words, TABLE)
        idx6 = load_list("idx6", offs6)
        load_plane(vs_plane, vs_scales)
        idx7 = load_list("idx7", offs7)

        for q in range(QUADRANTS):
            nc.vector.tensor_copy(
                wt_plane[32 * q : 32 * q + 4, :].bitcast(I32), wt_rows[:, q, :, :].rearrange("s i n -> s (i n)")
            )

        def cols(i):
            return slice(P * i, P * (i + 1))

        def half_list(offsets, h):
            return offsets[:, HALF * h : HALF * (h + 1)]

        def deal(copy, name, src, first, count, dtype, after=None):
            weights = src.shape[1] // HID
            tile = sbuf(name, weights * count * P, dtype, after)
            run = LINE if dtype == U8 else LINE // 4
            copy(
                tile[:].rearrange("p (w t c i) -> p w c t i", w=weights, t=count, i=run),
                src.rearrange("p (w c i t) -> p w c t i", w=weights, i=run, t=PACK)[:, :, :, first : first + count, :],
            )
            return tile

        boards = {}

        def second_product(t):
            b_ps = psum.tile([P, SLOTS], F32, name="b_ps%d" % t)
            nc.tensor.matmul_mx(
                out=b_ps[:], lhsT=w2_c[:, cols(t)].bitcast(E4M3), lhsT_scale=w2_s[t // 2][:, cols(t % 2)],
                rhs=xo_c[:].bitcast(E5M2), rhs_scale=xo_s[:], start=True, stop=True,
            )
            return b_ps

        def fetch_partner(t):
            b_sb = sbuf("b_sb%d" % t, WIDE, F32)
            nc.scalar.copy(b_sb[:, 0:SLOTS], b_banks[t][:])
            nc.scalar.activation(picked[t], b_sb[:].indirect(idx3[:]), COPY, scale=sa_t[:, t : t + 1])

        def fetch_last_partner(t):
            b_sb = sbuf("b_sb%d" % t, SLOTS, F32, "xt_plane")
            nc.vector.tensor_copy(b_sb[:], b_banks[t][:])
            for h in range(2):
                nc.scalar.activation(
                    picked[t][:, cols(h)], b_sb[:].indirect(half_list(idx3, h)), COPY, scale=sa_t[:, t : t + 1]
                )

        board_after = (None, "xt_all", "xt_plane", "kept0")

        def first_result(pair, pair_s):
            for t in (2 * pair, 2 * pair + 1):
                a_ps = psum.tile([P, SLOTS], F32, name="a_ps%d" % t)
                nc.tensor.matmul_mx(
                    out=a_ps[:], lhsT=w0_c[:, cols(t)].bitcast(E4M3), lhsT_scale=pair_s[:, cols(2 + t % 2)],
                    rhs=xo_c[:].bitcast(E5M2), rhs_scale=xo_s[:], start=True, stop=False,
                )
                nc.tensor.matmul_mx(
                    out=a_ps[:], lhsT=w_c[:, cols(t)].bitcast(E5M2), lhsT_scale=pair_s[:, cols(t % 2)],
                    rhs=xt_c[:].bitcast(E2M1), rhs_scale=xt_s[:], start=False, stop=True,
                )
                kept = sbuf("kept%d" % t, SLOTS, F32)
                nc.vector.tensor_tensor(kept[:], a_ps[:], picked[t], MAX)
                boards[t] = sbuf("board%d" % t, BOARD, F32, board_after[t])
                zeroing = nc.vector if board_after[t] is None else nc.gpsimd
                zeroing.memset(boards[t][:].bitcast(I32), 0)
                nc.scalar.activation(boards[t][:].indirect(idx4[:]), kept[:], COPY)

        w2_s = [deal(nc.vector.tensor_copy, "w2_s0", wt_plane[:, 0:HID], 0, 2, U8)]
        xo_c = gather("xo_c", xo_all[:].bitcast(U32), idx2, U32)
        xo_s = gather("xo_s", xo_plane[:], idx2, U8)
        w2_s.append(deal(nc.vector.tensor_copy, "w2_s1", wt_plane[:, 0:HID], 2, 2, U8, "xo_plane"))
        w2_c = deal(nc.scalar.copy, "w2_c", w2_raw[:].bitcast(U32), 0, PACK, U32)
        w0_c = deal(nc.scalar.copy, "w0_c0", w0_raw[:].bitcast(U32), 0, PACK, U32)
        lower_s = deal(nc.vector.tensor_copy, "both_s0", wt_plane[:, HID : 3 * HID], 0, 2, U8)
        w_c = deal(nc.vector.tensor_copy, "w_c", w_raw[:], 0, PACK, I32)

        picked_first = sbuf("picked_first", SLOTS, F32, "w0_raw")
        picked_rest = sbuf("picked_rest", (PACK - 1) * SLOTS, F32, "w_raw")
        picked = [picked_first[:]] + [picked_rest[:, SLOTS * i : SLOTS * (i + 1)] for i in range(PACK - 1)]
        b_banks = [second_product(t) for t in range(PACK)]
        for t in range(PACK - 1):
            fetch_partner(t)
        xt_c = gather("xt_c", xt_all[:], idx, U16)
        xt_s = gather("xt_s", xt_plane[:], idx, U8)
        fetch_last_partner(PACK - 1)
        first_result(0, lower_s)

        upper_s = deal(nc.vector.tensor_copy, "both_s1", wt_plane[:, HID : 3 * HID], 2, 2, U8, "w0_raw")
        first_result(1, upper_s)

        vs_s = gather("vs_s", vs_plane[:], idx6, U8, "both_s0")
        vs_c = gather("vs_c", vs_all[:].bitcast(U32), idx6, U32, "vs_plane")
        pages = []
        for nb in range(2):
            page = sbuf("page%d" % nb, PAGE, F32, "kept%d" % (nb + 1))
            nc.gpsimd.memset(page[:].bitcast(I32), 0)
            pages.append(page)

        last = PACK - 1
        hid = keep.tile([P, PACK, SLOTS], F32, name="hid", tag="vs_all", align_bytes=64)
        halves = [keep.tile([P, P, PACK], BF16, name="hid_bf%d" % h, align_bytes=64) for h in range(2)]
        for t in range(last):
            nc.vector.tensor_copy(hid[:, t, :], boards[t][:].indirect(idx5[:]))
        for h in range(2):
            nc.vector.tensor_copy(halves[h][:, :, 0:last], hid[:, 0:last, cols(h)].rearrange("p t o -> p o t"))
        nc.vector.tensor_copy(hid[:, last, :], boards[last][:].indirect(idx5[:]))
        for h in range(2):
            nc.vector.tensor_copy(halves[h][:, :, last], hid[:, last, cols(h)])

        codes = []
        for h in range(2):
            hid_c = sbuf("hid_c%d" % h, P, U32)
            hid_s = sbuf("hid_s%d" % h, P, U8)
            nc.vector.quantize_mx(
                out=hid_c[:].bitcast(E5M2), scales=hid_s[:], in_=halves[h][:].rearrange("p o t -> p (o t)")
            )
            codes.append((hid_c, hid_s))
        for h in range(2):
            hid_c, hid_s = codes[h]
            for nb in range(2):
                p_ps = psum.tile([P, P], F32, name="b_ps%d" % (2 * h + nb))
                nc.tensor.matmul_mx(
                    out=p_ps[:], lhsT=vs_c[:, cols(nb)].bitcast(E4M3), lhsT_scale=vs_s[:, cols(nb)],
                    rhs=hid_c[:].bitcast(E5M2), rhs_scale=hid_s[:], start=True, stop=True,
                )
                p_sb = sbuf("p_sb%d" % (2 * h + nb), P, F32)
                nc.vector.tensor_copy(p_sb[:], p_ps[:])
                nc.scalar.activation(pages[nb][:].indirect(half_list(idx7, h)), p_sb[:], COPY)
        for nb in range(2):
            nc.sync.dma_start(out[cols(nb), :], pages[nb][:])
